import numpy as np
import ml_dtypes


def mxq(x, axis, fmt="e4m3"):
    dtype, down = {"e4m3": (ml_dtypes.float8_e4m3fn, 7), "e5m2": (ml_dtypes.float8_e5m2, 14)}[fmt]
    v = np.moveaxis(np.asarray(x, np.float32).astype(ml_dtypes.bfloat16).astype(np.float64), axis, -1)
    blocks = v.reshape(v.shape[:-1] + (-1, 32))
    amax = np.abs(blocks).max(-1, keepdims=True)
    byte = np.maximum(np.where(amax > 0, np.frexp(amax)[1] - 1 + 127, 0) - down, 1)
    scale = np.exp2(byte - 127.0)
    codes = (blocks / scale).astype(np.float32).astype(dtype).astype(np.float64)
    return np.moveaxis((codes * scale).reshape(v.shape), -1, axis)


WIDE = False


def mx_kscale(k):
    if not WIDE:
        return np.ones(k)
    levels = np.array([30, -30])
    if k % 512:
        return np.exp2(np.random.permutation(np.resize(levels, k // 32))).repeat(32)
    a = np.empty((k // 512, 16))
    for p in range(k // 512):
        a[p, :8] = np.random.permutation(np.resize(levels, 8))
        for g in range(8):
            far = levels[np.abs(levels - a[p, g]) >= 10]
            a[p, g + 8] = far[np.random.randint(len(far))]
    return np.exp2(a.ravel()).repeat(32)


def f64(x):
    return np.asarray(x).astype(np.float64)


def striped(idx):
    return np.tile(np.asarray(idx).reshape(-1, 16).T, (8, 1)).astype(np.uint16)


def unstriped(offs):
    return offs[:16].T.reshape(-1).astype(np.int64)


E2M1 = np.array([0.0, 0.5, 1.0, 1.5, 2.0, 3.0, 4.0, 6.0, -0.0, -0.5, -1.0, -1.5, -2.0, -3.0, -4.0, -6.0])


def pack_weight(w, fmt):
    k, n = w.shape
    w = f64(np.asarray(w, np.float32).astype(ml_dtypes.bfloat16)).reshape(k // 32, 32, n)
    amax = np.abs(w).max(1)
    if fmt in ("e4m3", "e5m2"):
        byte = np.frexp(amax)[1] - 1 + 127 - (7 if fmt == "e4m3" else 14)
    else:
        mant, ex = np.frexp(amax / 6.0)
        byte = np.where(mant > 0.5, ex, ex - 1) + 127
    byte = np.clip(np.where(amax > 0, byte, 1), 1, 254)
    scaled = (w * np.exp2(127.0 - byte)[:, None, :]).reshape(k, n).astype(np.float32)
    by_word = np.ascontiguousarray(scaled.reshape(k // 512, 128, 4, n).transpose(0, 1, 3, 2))
    if fmt in ("e4m3", "e5m2"):
        words = by_word.astype(ml_dtypes.float8_e4m3fn if fmt == "e4m3" else ml_dtypes.float8_e5m2).view(np.uint8)
    else:
        c = by_word.astype(ml_dtypes.float4_e2m1fn).view(np.uint8) & 0xF
        words = (c[..., 0::2] | (c[..., 1::2] << 4)).reshape(k // 512, 128, 2 * n)
    return np.ascontiguousarray(words), np.ascontiguousarray(byte.astype(np.uint8).reshape(k // 512, 16, n))


def unpack_weight(words, scales, fmt):
    g, _, n = scales.shape
    words = np.ascontiguousarray(words).reshape(g, 128, n, -1)
    if fmt in ("e4m3", "e5m2"):
        vals = words.view(ml_dtypes.float8_e4m3fn if fmt == "e4m3" else ml_dtypes.float8_e5m2).astype(np.float64)
    else:
        nib = np.empty((g, 128, n, 4), np.uint8)
        nib[..., 0::2] = words & 0xF
        nib[..., 1::2] = words >> 4
        vals = E2M1[nib]
    vals = vals * np.repeat(np.exp2(scales.astype(np.float64) - 127.0), 8, axis=1)[..., None]
    return vals.transpose(0, 1, 3, 2).reshape(g * 512, n)


K, T, J, N, C = 1024, 1024, 256, 256, 512


def setup_inputs():
    n = np.random.standard_normal
    idx = np.random.permutation(T)[:J]
    idx2 = np.random.permutation(C)[:N]
    fk = mx_kscale(K)
    xtp = pack_weight(n((K, T)) * np.random.uniform(0.4, 1.6, (1, T)) / fk[:, None], "e5m2")
    wap = pack_weight(n((K, N)) * 1 / np.sqrt(K) * fk[:, None], "e4m3")
    return {
        "xt_words": xtp[0],
        "xt_scales": xtp[1],
        "wa_words": wap[0],
        "wa_scales": wap[1],
        "wb": (n((K, N)) * 1 / np.sqrt(K) * fk[:, None]).astype(np.float32),
        "bi": (np.random.uniform(-0.6, 0.6, (1, N))).astype(np.float32),
        "tb": (1.0 * n((J, C))).astype(np.float32),
        "offs": striped(idx),
        "offs2": striped(idx2),
    }


def reference(xt_words, xt_scales, wa_words, wa_scales, wb, bi, tb, offs, offs2):
    idx = unstriped(offs)
    idx2 = unstriped(offs2)
    xtu = unpack_weight(xt_words, xt_scales, "e5m2")
    wau = unpack_weight(wa_words, wa_scales, "e4m3")
    xtidxg = xtu[:, idx]
    a = xtidxg.T @ wau
    wbq = mxq(f64(wb), 0, "e4m3")
    b0 = xtidxg.T @ wbq
    b2 = b0 + f64(bi)
    y = (a + 0.5 * b2) * f64(tb)[:, idx2]
    return y

@@ -1,0 +1,156 @@
+from contextlib import ExitStack
+
+import concourse.mybir as mybir
+from concourse.masks import make_identity
+
+K, T, J, N, C = 1024, 1024, 256, 256, 512
+FLOPS = 2 * 2 * J * N * K
+
+F32 = mybir.dt.float32
+BF16 = mybir.dt.bfloat16
+I32 = mybir.dt.int32
+U32 = mybir.dt.uint32
+U16 = mybir.dt.uint16
+U8 = mybir.dt.uint8
+E4M3X4 = mybir.dt.float8_e4m3fn_x4
+E5M2X4 = mybir.dt.float8_e5m2_x4
+MULT = mybir.AluOpType.mult
+ADD = mybir.AluOpType.add
+COPY = mybir.ActivationFunctionType.Copy
+
+P = 128
+PACK = 4
+PASSES = K // (P * PACK)
+SLOT_TILES = J // P
+QUADRANTS = 4
+QUADRANT = P // QUADRANTS
+LIST_ROWS = 16
+
+
+def tile_list_rows_onetoken_tablegate_kernel(
+    tc, xt_words, xt_scales, wa_words, wa_scales, wb, bi, tb, offs, offs2, out
+):
+    nc = tc.nc
+    with ExitStack() as ctx:
+        sb = ctx.enter_context(tc.tile_pool(name="sb", bufs=1))
+        ps = ctx.enter_context(tc.psum_pool(name="ps", bufs=1))
+
+        token_list = sb.tile([P, J // LIST_ROWS], U16, name="token_list")
+        entry_list = sb.tile([P, N // LIST_ROWS], U16, name="entry_list")
+        xt_scale_rows = sb.tile([P, PASSES, T], U8, name="xt_scale_rows", align_bytes=64)
+        wa_scale_rows = sb.tile([P, PASSES, N], U8, name="wa_scale_rows", align_bytes=64)
+        bias_pairs = sb.tile([P, N // P], F32, name="bias_pairs")
+        wb_rows = [sb.tile([P, PACK, N], F32, name="wb_rows%d" % z) for z in range(PASSES)]
+        xt_codes = [sb.tile([P, T], I32, name="xt_codes%d" % z) for z in range(PASSES)]
+        wa_codes = sb.tile([P, PASSES, N], I32, name="wa_codes", align_bytes=64)
+        tb_rows = [sb.tile([P, C], F32, name="tb_rows%d" % s) for s in range(SLOT_TILES)]
+
+        def load_scale_rows(queue, tile, scales, q):
+            queue.dma_start(
+                out=tile[QUADRANT * q : QUADRANT * q + PACK, :, :].bitcast(I32),
+                in_=scales[:, PACK * q : PACK * (q + 1), :].rearrange("z r c -> r z c").bitcast(I32),
+            )
+
+        def load_wb(z):
+            rows = wb[z * P * PACK : (z + 1) * P * PACK, :]
+            nc.sync.dma_start(out=wb_rows[z][:], in_=rows.rearrange("(p t) n -> p t n", t=PACK))
+
+        identity = sb.tile([P, P], F32, name="identity")
+        make_identity(nc, identity[:])
+        nc.vector.memset(xt_scale_rows[:].bitcast(I32), 0)
+
+        nc.sync.dma_start(token_list[:], offs)
+        nc.scalar.dma_start(out=bias_pairs[:], in_=bi[0, :].rearrange("(p m) -> p m", p=P))
+        load_wb(0)
+        load_wb(1)
+        for q in range(QUADRANTS):
+            load_scale_rows(nc.scalar if q < 2 else nc.sync, xt_scale_rows, xt_scales, q)
+        for z in range(PASSES):
+            nc.sync.dma_start(
+                out=xt_codes[z][:], in_=xt_words[z].rearrange("p c t -> p (c t)").bitcast(I32)
+            )
+        nc.sync.dma_start(entry_list[:], offs2)
+        nc.sync.dma_start(
+            out=wa_codes[:], in_=wa_words.rearrange("z p n t -> p z (n t)").bitcast(I32)
+        )
+        for s in range(SLOT_TILES):
+            nc.sync.dma_start(out=tb_rows[s][:], in_=tb[s * P : (s + 1) * P, :])
+        for q in range(QUADRANTS):
+            load_scale_rows(nc.gpsimd, wa_scale_rows, wa_scales, q)
+
+        bias_bank = ps.tile([P, N // P, P], F32, name="bias_bank")
+        for m in range(N // P):
+            nc.tensor.transpose(
+                bias_bank[:, m, :], bias_pairs[:, m : m + 1].to_broadcast([P, P]), identity[:]
+            )
+        half_bias = sb.tile([P, N], F32, name="half_bias")
+        nc.scalar.activation(
+            half_bias[:].rearrange("p (k m) -> p k m", m=N // P),
+            bias_bank[:].rearrange("p m k -> p k m"),
+            COPY,
+            scale=0.5,
+        )
+
+        wb_codes = sb.tile([P, PASSES, N], U32, name="wb_codes", align_bytes=64)
+        wb_scale_rows = sb.tile([P, PASSES, N], U8, name="wb_scale_rows", align_bytes=64)
+        x_scale_rows = sb.tile([P, PASSES, J], U8, name="x_scale_rows", align_bytes=64)
+        x_codes = sb.tile([P, PASSES, J], U32, name="x_codes", align_bytes=64)
+        wb_grouped = [
+            sb.tile([P, N, PACK], BF16, name="wb_grouped%d" % z, align_bytes=64) for z in range(PASSES)
+        ]
+        for z in range(PASSES):
+            nc.scalar.copy(
+                wb_grouped[z][:].rearrange("p (c i) t -> p c t i", i=PACK),
+                wb_rows[z][:].rearrange("p t (c i) -> p c t i", i=PACK),
+            )
+        for z in range(PASSES):
+            nc.vector.quantize_mx(
+                out=wb_codes[:, z, :].bitcast(E4M3X4),
+                scales=wb_scale_rows[:, z, :],
+                in_=wb_grouped[z][:].rearrange("p n t -> p (n t)"),
+            )
+            nc.vector.tensor_copy(x_scale_rows[:, z, :], xt_scale_rows[:, z, :].indirect(token_list[:]))
+
+        list_columns = P // LIST_ROWS
+        nc.vector.tensor_copy(x_codes[:, 0, :], xt_codes[0][:].bitcast(U32).indirect(token_list[:]))
+        for s in range(SLOT_TILES):
+            nc.vector.tensor_copy(
+                x_codes[:, 1, s * P : (s + 1) * P],
+                xt_codes[1][:].bitcast(U32).indirect(token_list[:, s * list_columns : (s + 1) * list_columns]),
+            )
+
+        a_banks = [ps.tile([P, N], F32, name="a_bank%d" % s) for s in range(SLOT_TILES)]
+        b_banks = [ps.tile([P, N], F32, name="b_bank%d" % s) for s in range(SLOT_TILES)]
+
+        def multiply(banks, codes, scale_rows, s, z):
+            slots = slice(s * P, (s + 1) * P)
+            nc.tensor.matmul_mx(
+                out=banks[s][:],
+                lhsT=x_codes[:, z, slots].bitcast(E5M2X4),
+                lhsT_scale=x_scale_rows[:, z, slots],
+                rhs=codes[:, z, :].bitcast(E4M3X4),
+                rhs_scale=scale_rows[:, z, :],
+                start=(z == 0),
+                stop=(z == PASSES - 1),
+            )
+
+        for z in range(PASSES):
+            for s in range(SLOT_TILES):
+                multiply(b_banks, wb_codes, wb_scale_rows, s, z)
+        for s in range(SLOT_TILES):
+            for z in range(PASSES):
+                multiply(a_banks, wa_codes, wa_scale_rows, s, z)
+
+        gates = [sb.tile([P, N], F32, name="gate%d" % s) for s in range(SLOT_TILES)]
+        half_b = [sb.tile([P, N], F32, name="half_b%d" % s) for s in range(SLOT_TILES)]
+        sums = [sb.tile([P, N], F32, name="sum%d" % s) for s in range(SLOT_TILES)]
+        results = [sb.tile([P, N], F32, name="result%d" % s) for s in range(SLOT_TILES)]
+        for s in range(SLOT_TILES):
+            nc.scalar.activation(gates[s][:], tb_rows[s][:].indirect(entry_list[:]), COPY)
+        for s in range(SLOT_TILES):
+            nc.vector.scalar_tensor_tensor(half_b[s][:], b_banks[s][:], 0.5, half_bias[:], MULT, ADD)
+        for s in range(SLOT_TILES):
+            nc.vector.tensor_tensor(sums[s][:], a_banks[s][:], half_b[s][:], ADD)
+        for s in range(SLOT_TILES):
+            nc.vector.tensor_tensor(results[s][:], sums[s][:], gates[s][:], MULT)
+            nc.sync.dma_start(out=out[s * P : (s + 1) * P, :], in_=results[s][:])

@@ -1,7 +1,6 @@
 from contextlib import ExitStack
 
 import concourse.mybir as mybir
-from concourse.masks import make_identity
 
 K, T, J, N, C = 1024, 1024, 256, 256, 512
 FLOPS = 2 * 2 * J * N * K
@@ -25,6 +24,7 @@ SLOT_TILES = J // P
 QUADRANTS = 4
 QUADRANT = P // QUADRANTS
 LIST_ROWS = 16
+BIAS_RUN = N // QUADRANT
 
 
 def tile_list_rows_onetoken_tablegate_kernel(
@@ -37,13 +37,11 @@ def tile_list_rows_onetoken_tablegate_kernel(
 
         token_list = sb.tile([P, J // LIST_ROWS], U16, name="token_list")
         entry_list = sb.tile([P, N // LIST_ROWS], U16, name="entry_list")
-        xt_scale_rows = sb.tile([P, PASSES, T], U8, name="xt_scale_rows", align_bytes=64)
-        wa_scale_rows = sb.tile([P, PASSES, N], U8, name="wa_scale_rows", align_bytes=64)
-        bias_pairs = sb.tile([P, N // P], F32, name="bias_pairs")
-        wb_rows = [sb.tile([P, PACK, N], F32, name="wb_rows%d" % z) for z in range(PASSES)]
-        xt_codes = [sb.tile([P, T], I32, name="xt_codes%d" % z) for z in range(PASSES)]
-        wa_codes = sb.tile([P, PASSES, N], I32, name="wa_codes", align_bytes=64)
-        tb_rows = [sb.tile([P, C], F32, name="tb_rows%d" % s) for s in range(SLOT_TILES)]
+
+        def staged(shape, dtype, name, slot):
+            return sb.tile(shape, dtype, name=name, tag="slot%d" % slot, align_bytes=64)
+
+        xt_scale_rows = staged([P, PASSES, T], U8, "xt_scale_rows", 5)
 
         def load_scale_rows(queue, tile, scales, q):
             queue.dma_start(
@@ -51,73 +49,98 @@ def tile_list_rows_onetoken_tablegate_kernel(
                 in_=scales[:, PACK * q : PACK * (q + 1), :].rearrange("z r c -> r z c").bitcast(I32),
             )
 
-        def load_wb(z):
-            rows = wb[z * P * PACK : (z + 1) * P * PACK, :]
-            nc.sync.dma_start(out=wb_rows[z][:], in_=rows.rearrange("(p t) n -> p t n", t=PACK))
-
-        identity = sb.tile([P, P], F32, name="identity")
-        make_identity(nc, identity[:])
         nc.vector.memset(xt_scale_rows[:].bitcast(I32), 0)
-
+        bias_runs = staged([P, BIAS_RUN], F32, "bias_runs", 0)
+        nc.scalar.dma_start(
+            out=bias_runs[:],
+            in_=bi.rearrange("o (k b) -> o k b", k=QUADRANT).to_broadcast([QUADRANTS, QUADRANT, BIAS_RUN]),
+        )
         nc.sync.dma_start(token_list[:], offs)
-        nc.scalar.dma_start(out=bias_pairs[:], in_=bi[0, :].rearrange("(p m) -> p m", p=P))
-        load_wb(0)
-        load_wb(1)
         for q in range(QUADRANTS):
-            load_scale_rows(nc.scalar if q < 2 else nc.sync, xt_scale_rows, xt_scales, q)
-        for z in range(PASSES):
-            nc.sync.dma_start(
-                out=xt_codes[z][:], in_=xt_words[z].rearrange("p c t -> p (c t)").bitcast(I32)
-            )
+            load_scale_rows(nc.scalar, xt_scale_rows, xt_scales, q)
+
+        def load_wb(z, slot):
+            tile = staged([P, PACK, N], F32, "wb_rows%d" % z, slot)
+            rows = wb[z * P * PACK : (z + 1) * P * PACK, :]
+            nc.sync.dma_start(out=tile[:], in_=rows.rearrange("(p t) n -> p t n", t=PACK))
+            return tile
+
+        def load_xt(z, slot):
+            tile = staged([P, T], I32, "xt_codes%d" % z, slot)
+            nc.sync.dma_start(out=tile[:], in_=xt_words[z].rearrange("p c t -> p (c t)").bitcast(I32))
+            return tile
+
+        def load_tb(s, slot):
+            tile = staged([P, C], F32, "tb_rows%d" % s, slot)
+            nc.sync.dma_start(out=tile[:], in_=tb[s * P : (s + 1) * P, :])
+            return tile
+
+        xt_codes0 = load_xt(0, 3)
+        wb_rows0 = load_wb(0, 4)
         nc.sync.dma_start(entry_list[:], offs2)
+
+        bias_blocks = staged([P, BIAS_RUN, QUADRANT], F32, "bias_blocks", 1)
+        bias_turned = staged([P, BIAS_RUN, QUADRANT], F32, "bias_turned", 2)
+        half_bias = sb.tile([P, N], F32, name="half_bias")
+        nc.vector.tensor_scalar_mul(
+            bias_blocks[:], bias_runs[:].unsqueeze(2).to_broadcast([P, BIAS_RUN, QUADRANT]), 0.5
+        )
+        nc.vector.transpose(
+            bias_turned[:].rearrange("p b k -> p (b k)"), bias_blocks[:].rearrange("p b i -> p (b i)")
+        )
+        nc.vector.tensor_copy(
+            half_bias[:].rearrange("p (k b) -> p k b", b=BIAS_RUN), bias_turned[:].rearrange("p b k -> p k b")
+        )
+
+        wb_rows1 = load_wb(1, 0)
+        xt_codes1 = load_xt(1, 1)
+        wa_codes = staged([P, PASSES, N], I32, "wa_codes", 2)
         nc.sync.dma_start(
             out=wa_codes[:], in_=wa_words.rearrange("z p n t -> p z (n t)").bitcast(I32)
-        )
-        for s in range(SLOT_TILES):
-            nc.sync.dma_start(out=tb_rows[s][:], in_=tb[s * P : (s + 1) * P, :])
-        for q in range(QUADRANTS):
-            load_scale_rows(nc.gpsimd, wa_scale_rows, wa_scales, q)
-
-        bias_bank = ps.tile([P, N // P, P], F32, name="bias_bank")
-        for m in range(N // P):
-            nc.tensor.transpose(
-                bias_bank[:, m, :], bias_pairs[:, m : m + 1].to_broadcast([P, P]), identity[:]
-            )
-        half_bias = sb.tile([P, N], F32, name="half_bias")
-        nc.scalar.activation(
-            half_bias[:].rearrange("p (k m) -> p k m", m=N // P),
-            bias_bank[:].rearrange("p m k -> p k m"),
-            COPY,
-            scale=0.5,
         )
 
         wb_codes = sb.tile([P, PASSES, N], U32, name="wb_codes", align_bytes=64)
         wb_scale_rows = sb.tile([P, PASSES, N], U8, name="wb_scale_rows", align_bytes=64)
         x_scale_rows = sb.tile([P, PASSES, J], U8, name="x_scale_rows", align_bytes=64)
-        x_codes = sb.tile([P, PASSES, J], U32, name="x_codes", align_bytes=64)
-        wb_grouped = [
-            sb.tile([P, N, PACK], BF16, name="wb_grouped%d" % z, align_bytes=64) for z in range(PASSES)
-        ]
-        for z in range(PASSES):
-            nc.scalar.copy(
-                wb_grouped[z][:].rearrange("p (c i) t -> p c t i", i=PACK),
-                wb_rows[z][:].rearrange("p t (c i) -> p c t i", i=PACK),
+        x_codes0 = sb.tile([P, J], U32, name="x_codes0", align_bytes=64)
+        wb_grouped0 = sb.tile([P, N, PACK], BF16, name="wb_grouped0", align_bytes=64)
+        wb_grouped1 = staged([P, N, PACK], BF16, "wb_grouped1", 6)
+
+        def round_and_group(copy, grouped, rows, columns):
+            copy(
+                grouped[:, columns, :].rearrange("p (c i) t -> p c t i", i=PACK),
+                rows[:, :, columns].rearrange("p t (c i) -> p c t i", i=PACK),
             )
-        for z in range(PASSES):
+
+        def quantise_wb(z, grouped):
             nc.vector.quantize_mx(
                 out=wb_codes[:, z, :].bitcast(E4M3X4),
                 scales=wb_scale_rows[:, z, :],
-                in_=wb_grouped[z][:].rearrange("p n t -> p (n t)"),
+                in_=grouped[:].rearrange("p n t -> p (n t)"),
             )
-            nc.vector.tensor_copy(x_scale_rows[:, z, :], xt_scale_rows[:, z, :].indirect(token_list[:]))
 
+        nc.vector.tensor_copy(x_codes0[:], xt_codes0[:].bitcast(U32).indirect(token_list[:]))
+        wa_scale_rows = staged([P, PASSES, N], U8, "wa_scale_rows", 3)
+        for q in range(QUADRANTS):
+            load_scale_rows(nc.sync, wa_scale_rows, wa_scales, q)
+        round_and_group(nc.vector.tensor_copy, wb_grouped0, wb_rows0, slice(0, N // 2))
+        round_and_group(nc.scalar.copy, wb_grouped0, wb_rows0, slice(N // 2, N))
+        for z in range(PASSES):
+            nc.vector.tensor_copy(x_scale_rows[:, z, :], xt_scale_rows[:, z, :].indirect(token_list[:]))
+        tb_rows = [load_tb(0, 4), load_tb(1, 5)]
+        quantise_wb(0, wb_grouped0)
+        round_and_group(nc.scalar.copy, wb_grouped1, wb_rows1, slice(0, N))
         list_columns = P // LIST_ROWS
-        nc.vector.tensor_copy(x_codes[:, 0, :], xt_codes[0][:].bitcast(U32).indirect(token_list[:]))
-        for s in range(SLOT_TILES):
-            nc.vector.tensor_copy(
-                x_codes[:, 1, s * P : (s + 1) * P],
-                xt_codes[1][:].bitcast(U32).indirect(token_list[:, s * list_columns : (s + 1) * list_columns]),
-            )
+
+        def gather_last_words(s, slot):
+            tile = staged([P, P], U32, "x_codes1_%d" % s, slot)
+            entries = token_list[:, s * list_columns : (s + 1) * list_columns]
+            nc.vector.tensor_copy(tile[:], xt_codes1[:].bitcast(U32).indirect(entries))
+            return tile
+
+        x_codes1 = [gather_last_words(0, 7)]
+        quantise_wb(1, wb_grouped1)
+        x_codes1.append(gather_last_words(1, 6))
 
         a_banks = [ps.tile([P, N], F32, name="a_bank%d" % s) for s in range(SLOT_TILES)]
         b_banks = [ps.tile([P, N], F32, name="b_bank%d" % s) for s in range(SLOT_TILES)]
@@ -126,7 +149,7 @@ def tile_list_rows_onetoken_tablegate_kernel(
             slots = slice(s * P, (s + 1) * P)
             nc.tensor.matmul_mx(
                 out=banks[s][:],
-                lhsT=x_codes[:, z, slots].bitcast(E5M2X4),
+                lhsT=(x_codes0[:, slots] if z == 0 else x_codes1[s][:]).bitcast(E5M2X4),
                 lhsT_scale=x_scale_rows[:, z, slots],
                 rhs=codes[:, z, :].bitcast(E4M3X4),
                 rhs_scale=scale_rows[:, z, :],
@@ -134,12 +157,12 @@ def tile_list_rows_onetoken_tablegate_kernel(
                 stop=(z == PASSES - 1),
             )
 
-        for z in range(PASSES):
-            for s in range(SLOT_TILES):
-                multiply(b_banks, wb_codes, wb_scale_rows, s, z)
         for s in range(SLOT_TILES):
-            for z in range(PASSES):
-                multiply(a_banks, wa_codes, wa_scale_rows, s, z)
+            multiply(b_banks, wb_codes, wb_scale_rows, s, 0)
+        for s in range(SLOT_TILES):
+            multiply(a_banks, wa_codes, wa_scale_rows, s, 0)
+            multiply(b_banks, wb_codes, wb_scale_rows, s, 1)
+            multiply(a_banks, wa_codes, wa_scale_rows, s, 1)
 
         gates = [sb.tile([P, N], F32, name="gate%d" % s) for s in range(SLOT_TILES)]
         half_b = [sb.tile([P, N], F32, name="half_b%d" % s) for s in range(SLOT_TILES)]
@@ -147,10 +170,14 @@ def tile_list_rows_onetoken_tablegate_kernel(
         results = [sb.tile([P, N], F32, name="result%d" % s) for s in range(SLOT_TILES)]
         for s in range(SLOT_TILES):
             nc.scalar.activation(gates[s][:], tb_rows[s][:].indirect(entry_list[:]), COPY)
-        for s in range(SLOT_TILES):
-            nc.vector.scalar_tensor_tensor(half_b[s][:], b_banks[s][:], 0.5, half_bias[:], MULT, ADD)
-        for s in range(SLOT_TILES):
-            nc.vector.tensor_tensor(sums[s][:], a_banks[s][:], half_b[s][:], ADD)
-        for s in range(SLOT_TILES):
-            nc.vector.tensor_tensor(results[s][:], sums[s][:], gates[s][:], MULT)
-            nc.sync.dma_start(out=out[s * P : (s + 1) * P, :], in_=results[s][:])
+        halves = (slice(0, N // 2), slice(N // 2, N))
+        nc.vector.scalar_tensor_tensor(half_b[0][:], b_banks[0][:], 0.5, half_bias[:], MULT, ADD)
+        nc.vector.tensor_tensor(sums[0][:], a_banks[0][:], half_b[0][:], ADD)
+        nc.vector.scalar_tensor_tensor(half_b[1][:], b_banks[1][:], 0.5, half_bias[:], MULT, ADD)
+        nc.vector.tensor_tensor(results[0][:], sums[0][:], gates[0][:], MULT)
+        nc.sync.dma_start(out=out[0:P, :], in_=results[0][:])
+        for columns in halves:
+            nc.vector.tensor_tensor(sums[1][:, columns], a_banks[1][:, columns], half_b[1][:, columns], ADD)
+        for columns in halves:
+            nc.vector.tensor_tensor(results[1][:, columns], sums[1][:, columns], gates[1][:, columns], MULT)
+        nc.sync.dma_start(out=out[P : 2 * P, :], in_=results[1][:])

from contextlib import ExitStack

import concourse.mybir as mybir

K, T, J, N, C = 1024, 1024, 256, 256, 512
FLOPS = 2 * 2 * J * N * K

F32 = mybir.dt.float32
BF16 = mybir.dt.bfloat16
I32 = mybir.dt.int32
U32 = mybir.dt.uint32
U16 = mybir.dt.uint16
U8 = mybir.dt.uint8
E4M3X4 = mybir.dt.float8_e4m3fn_x4
E5M2X4 = mybir.dt.float8_e5m2_x4
MULT = mybir.AluOpType.mult
ADD = mybir.AluOpType.add
COPY = mybir.ActivationFunctionType.Copy

P = 128
PACK = 4
PASSES = K // (P * PACK)
SLOT_TILES = J // P
QUADRANTS = 4
QUADRANT = P // QUADRANTS
LIST_ROWS = 16
BIAS_RUN = N // QUADRANT


def tile_list_rows_onetoken_tablegate_kernel(
    tc, xt_words, xt_scales, wa_words, wa_scales, wb, bi, tb, offs, offs2, out
):
    nc = tc.nc
    with ExitStack() as ctx:
        sb = ctx.enter_context(tc.tile_pool(name="sb", bufs=1))
        ps = ctx.enter_context(tc.psum_pool(name="ps", bufs=1))

        token_list = sb.tile([P, J // LIST_ROWS], U16, name="token_list")
        entry_list = sb.tile([P, N // LIST_ROWS], U16, name="entry_list")

        def staged(shape, dtype, name, slot):
            return sb.tile(shape, dtype, name=name, tag="slot%d" % slot, align_bytes=64)

        xt_scale_rows = staged([P, PASSES, T], U8, "xt_scale_rows", 5)

        def load_scale_rows(queue, tile, scales, q):
            queue.dma_start(
                out=tile[QUADRANT * q : QUADRANT * q + PACK, :, :].bitcast(I32),
                in_=scales[:, PACK * q : PACK * (q + 1), :].rearrange("z r c -> r z c").bitcast(I32),
            )

        nc.vector.memset(xt_scale_rows[:].bitcast(I32), 0)
        bias_runs = staged([P, BIAS_RUN], F32, "bias_runs", 0)
        nc.scalar.dma_start(
            out=bias_runs[:],
            in_=bi.rearrange("o (k b) -> o k b", k=QUADRANT).to_broadcast([QUADRANTS, QUADRANT, BIAS_RUN]),
        )
        nc.sync.dma_start(token_list[:], offs)
        for q in range(QUADRANTS):
            load_scale_rows(nc.scalar, xt_scale_rows, xt_scales, q)

        def load_wb(z, slot):
            tile = staged([P, PACK, N], F32, "wb_rows%d" % z, slot)
            rows = wb[z * P * PACK : (z + 1) * P * PACK, :]
            nc.sync.dma_start(out=tile[:], in_=rows.rearrange("(p t) n -> p t n", t=PACK))
            return tile

        def load_xt(z, slot):
            tile = staged([P, T], I32, "xt_codes%d" % z, slot)
            nc.sync.dma_start(out=tile[:], in_=xt_words[z].rearrange("p c t -> p (c t)").bitcast(I32))
            return tile

        def load_tb(s, slot):
            tile = staged([P, C], F32, "tb_rows%d" % s, slot)
            nc.sync.dma_start(out=tile[:], in_=tb[s * P : (s + 1) * P, :])
            return tile

        xt_codes0 = load_xt(0, 3)
        wb_rows0 = load_wb(0, 4)
        nc.sync.dma_start(entry_list[:], offs2)

        bias_blocks = staged([P, BIAS_RUN, QUADRANT], F32, "bias_blocks", 1)
        bias_turned = staged([P, BIAS_RUN, QUADRANT], F32, "bias_turned", 2)
        half_bias = sb.tile([P, N], F32, name="half_bias")
        nc.vector.tensor_scalar_mul(
            bias_blocks[:], bias_runs[:].unsqueeze(2).to_broadcast([P, BIAS_RUN, QUADRANT]), 0.5
        )
        nc.vector.transpose(
            bias_turned[:].rearrange("p b k -> p (b k)"), bias_blocks[:].rearrange("p b i -> p (b i)")
        )
        nc.vector.tensor_copy(
            half_bias[:].rearrange("p (k b) -> p k b", b=BIAS_RUN), bias_turned[:].rearrange("p b k -> p k b")
        )

        wb_rows1 = load_wb(1, 0)
        xt_codes1 = load_xt(1, 1)
        wa_codes = staged([P, PASSES, N], I32, "wa_codes", 2)
        nc.sync.dma_start(
            out=wa_codes[:], in_=wa_words.rearrange("z p n t -> p z (n t)").bitcast(I32)
        )

        wb_codes = sb.tile([P, PASSES, N], U32, name="wb_codes", align_bytes=64)
        wb_scale_rows = sb.tile([P, PASSES, N], U8, name="wb_scale_rows", align_bytes=64)
        x_scale_rows = sb.tile([P, PASSES, J], U8, name="x_scale_rows", align_bytes=64)
        x_codes0 = sb.tile([P, J], U32, name="x_codes0", align_bytes=64)
        wb_grouped0 = sb.tile([P, N, PACK], BF16, name="wb_grouped0", align_bytes=64)
        wb_grouped1 = staged([P, N, PACK], BF16, "wb_grouped1", 6)

        def round_and_group(copy, grouped, rows, columns):
            copy(
                grouped[:, columns, :].rearrange("p (c i) t -> p c t i", i=PACK),
                rows[:, :, columns].rearrange("p t (c i) -> p c t i", i=PACK),
            )

        def quantise_wb(z, grouped):
            nc.vector.quantize_mx(
                out=wb_codes[:, z, :].bitcast(E4M3X4),
                scales=wb_scale_rows[:, z, :],
                in_=grouped[:].rearrange("p n t -> p (n t)"),
            )

        nc.vector.tensor_copy(x_codes0[:], xt_codes0[:].bitcast(U32).indirect(token_list[:]))
        wa_scale_rows = staged([P, PASSES, N], U8, "wa_scale_rows", 3)
        for q in range(QUADRANTS):
            load_scale_rows(nc.sync, wa_scale_rows, wa_scales, q)
        round_and_group(nc.vector.tensor_copy, wb_grouped0, wb_rows0, slice(0, N // 2))
        round_and_group(nc.scalar.copy, wb_grouped0, wb_rows0, slice(N // 2, N))
        for z in range(PASSES):
            nc.vector.tensor_copy(x_scale_rows[:, z, :], xt_scale_rows[:, z, :].indirect(token_list[:]))
        tb_rows = [load_tb(0, 4), load_tb(1, 5)]
        quantise_wb(0, wb_grouped0)
        round_and_group(nc.scalar.copy, wb_grouped1, wb_rows1, slice(0, N))
        list_columns = P // LIST_ROWS

        def gather_last_words(s, slot):
            tile = staged([P, P], U32, "x_codes1_%d" % s, slot)
            entries = token_list[:, s * list_columns : (s + 1) * list_columns]
            nc.vector.tensor_copy(tile[:], xt_codes1[:].bitcast(U32).indirect(entries))
            return tile

        x_codes1 = [gather_last_words(0, 7)]
        quantise_wb(1, wb_grouped1)
        x_codes1.append(gather_last_words(1, 6))

        a_banks = [ps.tile([P, N], F32, name="a_bank%d" % s) for s in range(SLOT_TILES)]
        b_banks = [ps.tile([P, N], F32, name="b_bank%d" % s) for s in range(SLOT_TILES)]

        def multiply(banks, codes, scale_rows, s, z):
            slots = slice(s * P, (s + 1) * P)
            nc.tensor.matmul_mx(
                out=banks[s][:],
                lhsT=(x_codes0[:, slots] if z == 0 else x_codes1[s][:]).bitcast(E5M2X4),
                lhsT_scale=x_scale_rows[:, z, slots],
                rhs=codes[:, z, :].bitcast(E4M3X4),
                rhs_scale=scale_rows[:, z, :],
                start=(z == 0),
                stop=(z == PASSES - 1),
            )

        for s in range(SLOT_TILES):
            multiply(b_banks, wb_codes, wb_scale_rows, s, 0)
        for s in range(SLOT_TILES):
            multiply(a_banks, wa_codes, wa_scale_rows, s, 0)
            multiply(b_banks, wb_codes, wb_scale_rows, s, 1)
            multiply(a_banks, wa_codes, wa_scale_rows, s, 1)

        gates = [sb.tile([P, N], F32, name="gate%d" % s) for s in range(SLOT_TILES)]
        half_b = [sb.tile([P, N], F32, name="half_b%d" % s) for s in range(SLOT_TILES)]
        sums = [sb.tile([P, N], F32, name="sum%d" % s) for s in range(SLOT_TILES)]
        results = [sb.tile([P, N], F32, name="result%d" % s) for s in range(SLOT_TILES)]
        for s in range(SLOT_TILES):
            nc.scalar.activation(gates[s][:], tb_rows[s][:].indirect(entry_list[:]), COPY)
        halves = (slice(0, N // 2), slice(N // 2, N))
        nc.vector.scalar_tensor_tensor(half_b[0][:], b_banks[0][:], 0.5, half_bias[:], MULT, ADD)
        nc.vector.tensor_tensor(sums[0][:], a_banks[0][:], half_b[0][:], ADD)
        nc.vector.scalar_tensor_tensor(half_b[1][:], b_banks[1][:], 0.5, half_bias[:], MULT, ADD)
        nc.vector.tensor_tensor(results[0][:], sums[0][:], gates[0][:], MULT)
        nc.sync.dma_start(out=out[0:P, :], in_=results[0][:])
        for columns in halves:
            nc.vector.tensor_tensor(sums[1][:, columns], a_banks[1][:, columns], half_b[1][:, columns], ADD)
        for columns in halves:
            nc.vector.tensor_tensor(results[1][:, columns], sums[1][:, columns], gates[1][:, columns], MULT)
        nc.sync.dma_start(out=out[P : 2 * P, :], in_=results[1][:])
